import numpy as np
import ml_dtypes


def mxq(x, axis, fmt="e4m3"):
    dtype, down = {"e4m3": (ml_dtypes.float8_e4m3fn, 7), "e5m2": (ml_dtypes.float8_e5m2, 14)}[fmt]
    v = np.moveaxis(np.asarray(x, np.float32).astype(ml_dtypes.bfloat16).astype(np.float64), axis, -1)
    blocks = v.reshape(v.shape[:-1] + (-1, 32))
    amax = np.abs(blocks).max(-1, keepdims=True)
    byte = np.maximum(np.where(amax > 0, np.frexp(amax)[1] - 1 + 127, 0) - down, 1)
    scale = np.exp2(byte - 127.0)
    codes = (blocks / scale).astype(np.float32).astype(dtype).astype(np.float64)
    return np.moveaxis((codes * scale).reshape(v.shape), -1, axis)


WIDE = False


def mx_kscale(k):
    if not WIDE:
        return np.ones(k)
    levels = np.array([10, -10, 5, -5, 0])
    if k % 512:
        return np.exp2(np.random.permutation(np.resize(levels, k // 32))).repeat(32)
    a = np.empty((k // 512, 16))
    for p in range(k // 512):
        a[p, :8] = np.random.permutation(np.resize(levels, 8))
        for g in range(8):
            far = levels[np.abs(levels - a[p, g]) >= 10]
            a[p, g + 8] = far[np.random.randint(len(far))]
    return np.exp2(a.ravel()).repeat(32)


def f64(x):
    return np.asarray(x).astype(np.float64)


def striped(idx):
    return np.tile(np.asarray(idx).reshape(-1, 16).T, (8, 1)).astype(np.uint16)


def unstriped(offs):
    return offs[:16].T.reshape(-1).astype(np.int64)


E2M1 = np.array([0.0, 0.5, 1.0, 1.5, 2.0, 3.0, 4.0, 6.0, -0.0, -0.5, -1.0, -1.5, -2.0, -3.0, -4.0, -6.0])


def pack_weight(w, fmt):
    k, n = w.shape
    w = f64(np.asarray(w, np.float32).astype(ml_dtypes.bfloat16)).reshape(k // 32, 32, n)
    amax = np.abs(w).max(1)
    if fmt == "e4m3":
        byte = np.frexp(amax)[1] - 1 + 127 - 7
    else:
        mant, ex = np.frexp(amax / 6.0)
        byte = np.where(mant > 0.5, ex, ex - 1) + 127
    byte = np.clip(np.where(amax > 0, byte, 1), 1, 254)
    scaled = (w * np.exp2(127.0 - byte)[:, None, :]).reshape(k, n).astype(np.float32)
    by_word = np.ascontiguousarray(scaled.reshape(k // 512, 128, 4, n).transpose(0, 1, 3, 2))
    if fmt == "e4m3":
        words = by_word.astype(ml_dtypes.float8_e4m3fn).view(np.uint8)
    else:
        c = by_word.astype(ml_dtypes.float4_e2m1fn).view(np.uint8) & 0xF
        words = (c[..., 0::2] | (c[..., 1::2] << 4)).reshape(k // 512, 128, 2 * n)
    return np.ascontiguousarray(words), np.ascontiguousarray(byte.astype(np.uint8).reshape(k // 512, 16, n))


def unpack_weight(words, scales, fmt):
    g, _, n = scales.shape
    words = np.ascontiguousarray(words).reshape(g, 128, n, -1)
    if fmt == "e4m3":
        vals = words.view(ml_dtypes.float8_e4m3fn).astype(np.float64)
    else:
        nib = np.empty((g, 128, n, 4), np.uint8)
        nib[..., 0::2] = words & 0xF
        nib[..., 1::2] = words >> 4
        vals = E2M1[nib]
    vals = vals * np.repeat(np.exp2(scales.astype(np.float64) - 127.0), 8, axis=1)[..., None]
    return vals.transpose(0, 1, 3, 2).reshape(g * 512, n)


def bf(x):
    return np.asarray(x, np.float32).astype(ml_dtypes.bfloat16)


def planes(Y):
    r, m = Y.shape
    b = f64(bf(Y)).reshape(r // 32, 32, m)
    amax = np.abs(b).max(1)
    byte = np.clip(np.where(amax > 0, np.frexp(amax)[1] - 1 + 127 - 7, 1), 1, 254)
    codes = (b * np.exp2(127.0 - byte)[:, None, :]).reshape(r, m).astype(np.float32).astype(ml_dtypes.float8_e4m3fn).view(np.uint8)
    words = codes.reshape(r // 512, 128, 4, m).transpose(0, 1, 3, 2)
    return np.ascontiguousarray(words), np.ascontiguousarray(byte.astype(np.uint8).reshape(r // 512, 16, m))


D, T, I, J, U, Z, E = 512, 2048, 512, 512, 1024, 1024, 512


def setup_inputs():
    n = np.random.standard_normal
    idx = np.random.permutation(T)[:I]
    idx2 = np.random.permutation(U)[:J]
    idx3 = np.random.permutation(Z)[:J]
    fd = mx_kscale(D)
    fi = mx_kscale(I)
    ti = np.ones(T)
    ti[idx] = fi
    keysp = pack_weight(n((D, T)) / fd[:, None], "e2m1")
    return {
        "keys_words": keysp[0],
        "keys_scales": keysp[1],
        "notes": (n((D, U)) * 1.0 / np.sqrt(D) * fd[:, None]).astype(np.float32),
        "users2": (n((D, Z)) * 1.0 / np.sqrt(D) * fd[:, None]).astype(np.float32),
        "rowf": (np.random.uniform(0.02, 0.08, (I, 1)) * fi[:, None]).astype(np.float32),
        "vals": (n((E, T)) / ti).astype(np.float32),
        "offs": striped(idx),
        "offs2": striped(idx2),
        "offs3": striped(idx3),
    }


def reference(keys_words, keys_scales, notes, users2, rowf, vals, offs, offs2, offs3):
    idx = unstriped(offs)
    idx2 = unstriped(offs2)
    idx3 = unstriped(offs3)
    keysu = unpack_weight(keys_words, keys_scales, "e2m1")
    keysidxg = keysu[:, idx]
    notesq = mxq(f64(notes), 0, "e4m3")
    g1 = keysidxg.T @ notesq
    users2idx3q = mxq(f64(users2)[:, idx3], 0, "e4m3")
    g2 = keysidxg.T @ users2idx3q
    g0 = np.maximum(g1[:, idx2], g2)
    gr1 = g0 * f64(rowf)
    vt1 = f64(vals)[:, idx].T
    vt1q = mxq(vt1, 0, "e4m3")
    gr1q = mxq(gr1, 0, "e4m3")
    o = vt1q.T @ gr1q
    words, scales = planes(o)
    return o, words, scales

@@ -1,0 +1,199 @@
+from contextlib import ExitStack
+
+import concourse.mybir as mybir
+from concourse.masks import make_identity
+
+D, T, I, J, U, Z, E = 512, 2048, 512, 512, 1024, 1024, 512
+FLOPS = 2 * D * I * U + 2 * D * I * J + 2 * I * E * J
+
+F32 = mybir.dt.float32
+BF16 = mybir.dt.bfloat16
+I32 = mybir.dt.int32
+U32 = mybir.dt.uint32
+U16 = mybir.dt.uint16
+U8 = mybir.dt.uint8
+FP8X4 = mybir.dt.float8_e4m3fn_x4
+FP4X4 = mybir.dt.float4_e2m1fn_x4
+COPY = mybir.ActivationFunctionType.Copy
+MAX = mybir.AluOpType.max
+MULT = mybir.AluOpType.mult
+
+P = 128
+PACK = 4
+BANK = 512
+SCALAR_NOTES = 256
+VECTOR_RESULT = 384
+
+
+def tile_attend_tab_wideandown_exchange_pl_kernel(
+    tc, keys_words, keys_scales, notes, users2, rowf, vals, offs, offs2, offs3, out_0, out_1, out_2
+):
+    nc = tc.nc
+    with ExitStack() as ctx:
+        lists = ctx.enter_context(tc.tile_pool(name="lists", bufs=1))
+        sb = ctx.enter_context(tc.tile_pool(name="sb", bufs=1))
+        psum = ctx.enter_context(tc.psum_pool(name="psum", bufs=4))
+        psum_once = ctx.enter_context(tc.psum_pool(name="psum_once", bufs=1))
+
+        def quantize(name, woven, width):
+            codes = sb.tile([P, width], U32, name=name + "_codes", align_bytes=64)
+            scales = sb.tile([P, width], U8, name=name + "_scales", align_bytes=64)
+            nc.vector.quantize_mx(out=codes[:].bitcast(FP8X4), scales=scales[:], in_=woven)
+            return codes, scales
+
+        token_list = lists.tile([P, I // 16], U16, name="token_list")
+        note_list = lists.tile([P, J // 16], U16, name="note_list")
+        user_list = lists.tile([P, J // 16], U16, name="user_list")
+        key_words = sb.tile([P, T], U16, name="key_words")
+        key_scales = sb.tile([P, T], U8, name="key_scales")
+        nc.vector.memset(key_scales[:].bitcast(I32), 0)
+        nc.sync.dma_start(out=key_words[:].bitcast(I32), in_=keys_words[0].bitcast(I32))
+        nc.sync.dma_start(token_list[:], offs)
+        for q in range(4):
+            nc.scalar.dma_start(
+                out=key_scales[32 * q : 32 * q + 4, :].bitcast(I32), in_=keys_scales[0, 4 * q : 4 * q + 4, :].bitcast(I32)
+            )
+        nc.sync.dma_start(user_list[:], offs3)
+        nc.sync.dma_start(note_list[:], offs2)
+        notes_by_row = notes.rearrange("(p t) u -> p t u", t=PACK)
+        users_by_row = users2.rearrange("(p t) z -> p t z", t=PACK)
+        notes_raw = [sb.tile([P, PACK, BANK], F32, name=f"notes_raw{h}") for h in range(U // BANK)]
+        users_raw = [sb.tile([P, Z], F32, name=f"users_raw{t}") for t in range(PACK)]
+        factors = sb.tile([P, PACK], F32, name="factors")
+        nc.sync.dma_start(out=notes_raw[0][:], in_=notes_by_row[:, :, :BANK])
+        nc.sync.dma_start(out=factors[:], in_=rowf.rearrange("(p r) o -> p (r o)", r=PACK))
+        nc.sync.dma_start(out=users_raw[0][:], in_=users_by_row[:, 0, :])
+        nc.sync.dma_start(out=notes_raw[1][:], in_=notes_by_row[:, :, BANK:])
+        for t in range(1, PACK):
+            nc.sync.dma_start(out=users_raw[t][:], in_=users_by_row[:, t, :])
+        vals_by_row = vals.rearrange("(m r) t -> m r t", r=PACK)
+        vals_raw = []
+        for r in range(PACK):
+            raw = sb.tile([P, T], F32, name=f"vals_raw{r}", tag=f"vals_raw{r}")
+            nc.sync.dma_start(out=raw[:], in_=vals_by_row[:, r, :])
+            vals_raw.append(raw)
+
+        identity = sb.tile([P, P], F32, name="identity")
+        make_identity(nc, identity[:])
+
+        picked_words = sb.tile([P, I], U16, name="picked_words")
+        nc.vector.tensor_copy(picked_words[:], key_words[:].indirect(token_list[:]))
+        dealt_words = sb.tile([P, PACK, P], U16, name="dealt_words", align_bytes=64)
+        nc.vector.tensor_copy(dealt_words[:], picked_words[:].rearrange("p (s r) -> p r s", r=PACK))
+        picked_scales = sb.tile([P, I], U8, name="picked_scales")
+        nc.vector.tensor_copy(picked_scales[:], key_scales[:].indirect(token_list[:]))
+        dealt_scales = sb.tile([P, PACK, P], U8, name="dealt_scales", align_bytes=64)
+        nc.vector.tensor_copy(dealt_scales[:], picked_scales[:].rearrange("p (s r) -> p r s", r=PACK))
+
+        def keys_product(r, codes, scales):
+            bank = psum.tile([P, BANK], F32, name="bank")
+            nc.tensor.matmul_mx(
+                out=bank[:],
+                lhsT=dealt_words[:, r, :].bitcast(FP4X4),
+                lhsT_scale=dealt_scales[:, r, :],
+                rhs=codes[:].bitcast(FP8X4),
+                rhs_scale=scales[:],
+                start=True,
+                stop=True,
+            )
+            return bank
+
+        wide = [sb.tile([P, U], F32, name=f"wide{r}") for r in range(PACK)]
+        users_picked = sb.tile([P, PACK, J], BF16, name="users_picked")
+        for h in range(U // BANK):
+            woven = sb.tile([P, BANK, PACK], BF16, name=f"notes_woven{h}", align_bytes=64)
+            turned = notes_raw[h][:].rearrange("p t u -> p u t")
+            split = SCALAR_NOTES if h == 0 else 0
+            if split:
+                nc.scalar.copy(woven[:, :split, :], turned[:, :split, :])
+            nc.vector.tensor_copy(woven[:, split:, :], turned[:, split:, :])
+            codes, scales = quantize(f"notes{h}", woven[:].rearrange("p u t -> p (u t)"), BANK)
+            nc.scalar.activation(users_picked[:, h, :], users_raw[h][:].indirect(user_list[:]), COPY)
+            for r in range(PACK):
+                bank = keys_product(r, codes, scales)
+                nc.scalar.copy(wide[r][:, h * BANK : (h + 1) * BANK], bank[:])
+
+        for t in range(2, PACK):
+            nc.vector.tensor_copy(users_picked[:, t, :], users_raw[t][:].indirect(user_list[:]))
+        users_woven = sb.tile([P, J, PACK], BF16, name="users_woven", align_bytes=64)
+        nc.vector.tensor_copy(users_woven[:], users_picked[:].rearrange("p t j -> p j t"))
+        user_codes, user_scales = quantize("users", users_woven[:].rearrange("p j t -> p (j t)"), J)
+
+        table_rows = sb.tile([P, PACK, J], BF16, name="table_rows")
+        for r in range(PACK):
+            looked_up = sb.tile([P, J], F32, name=f"looked_up{r}")
+            if r == PACK - 1:
+                nc.vector.tensor_copy(looked_up[:], wide[r][:].indirect(note_list[:]))
+            else:
+                nc.scalar.activation(looked_up[:], wide[r][:].indirect(note_list[:]), COPY)
+            bank = keys_product(r, user_codes, user_scales)
+            larger = sb.tile([P, J], F32, name=f"larger{r}")
+            nc.vector.tensor_tensor(larger[:], looked_up[:], bank[:], MAX)
+            nc.vector.tensor_scalar(table_rows[:, r, :], larger[:], factors[:, r : r + 1], None, MULT)
+        table_woven = sb.tile([P, J, PACK], BF16, name="table_woven", align_bytes=64)
+        nc.vector.tensor_copy(table_woven[:], table_rows[:].rearrange("p r j -> p j r"))
+        table_codes, table_scales = quantize("table", table_woven[:].rearrange("p j r -> p (j r)"), J)
+
+        val_operands = []
+        for r in range(PACK):
+            vals_picked = sb.tile([P, I], BF16, name=f"vals_picked{r}")
+            nc.scalar.activation(vals_picked[:], vals_raw[r][:].indirect(token_list[:]), COPY)
+            pairs = vals_picked[:].bitcast(F32)
+            turned = psum_once.tile([P, 2, P], F32, name=f"turned{r}", tag="three_banks" if r == 2 else "one_bank")
+            for u in range(2):
+                nc.tensor.transpose(turned[:, u, :], pairs[:, u : I // 2 : 2], identity[:])
+            vals_woven = sb.tile([P, P * PACK], BF16, name=f"vals_woven{r}", align_bytes=64)
+            nc.scalar.copy(
+                vals_woven[:].bitcast(F32).rearrange("p (m u) -> p m u", u=2),
+                turned[:].rearrange("p u m -> p m u"),
+            )
+            val_operands.append(quantize(f"vals{r}", vals_woven[:], P))
+
+        result = sb.tile([P, PACK, J], F32, name="result", tag=f"vals_raw{PACK - 1}")
+        out_by_row = out_0.rearrange("(m r) j -> m r j", r=PACK)
+        early = psum_once.tile([P, PACK - 1, BANK], F32, name="early", tag="three_banks")
+        for r in range(PACK):
+            val_codes, val_scales = val_operands[r]
+            parts = 2 if r == PACK - 1 else 1
+            width = J // parts
+            for part in range(parts):
+                cols = slice(part * width, (part + 1) * width)
+                if parts == 2:
+                    late = psum.tile([P, BANK], F32, name="bank")
+                    bank = late[:, :width]
+                else:
+                    bank = early[:, r, :]
+                nc.tensor.matmul_mx(
+                    out=bank,
+                    lhsT=val_codes[:].bitcast(FP8X4),
+                    lhsT_scale=val_scales[:],
+                    rhs=table_codes[:, cols].bitcast(FP8X4),
+                    rhs_scale=table_scales[:, cols],
+                    start=True,
+                    stop=True,
+                )
+                if r == 1 or (part == 0 and parts == 2):
+                    nc.vector.tensor_copy(result[:, r, cols], bank)
+                else:
+                    nc.scalar.copy(result[:, r, cols], bank)
+            nc.sync.dma_start(out=out_by_row[:, r, :], in_=result[:, r, :])
+
+        result_woven = sb.tile([P, J, PACK], BF16, name="result_woven", align_bytes=64)
+        result_turned = result[:].rearrange("p r j -> p j r")
+        result_codes = sb.tile([P, J], U32, name="result_codes", align_bytes=64)
+        result_scales = sb.tile([P, J], U8, name="result_scales", align_bytes=64)
+        nc.vector.tensor_copy(result_woven[:, :256, :], result_turned[:, :256, :])
+        nc.vector.tensor_copy(result_woven[:, 256:VECTOR_RESULT, :], result_turned[:, 256:VECTOR_RESULT, :])
+        nc.scalar.copy(result_woven[:, VECTOR_RESULT:, :], result_turned[:, VECTOR_RESULT:, :])
+        for part in range(2):
+            cols = slice(part * 256, (part + 1) * 256)
+            nc.vector.quantize_mx(
+                out=result_codes[:, cols].bitcast(FP8X4),
+                scales=result_scales[:, cols],
+                in_=result_woven[:, cols, :].rearrange("p j r -> p (j r)"),
+            )
+        nc.sync.dma_start(out=out_1[0].rearrange("p c r -> p (c r)").bitcast(I32), in_=result_codes[:].bitcast(I32))
+        for q in range(4):
+            nc.scalar.dma_start(
+                out=out_2[0, 4 * q : 4 * q + 4, :].bitcast(I32), in_=result_scales[32 * q : 32 * q + 4, :].bitcast(I32)
+            )

@@ -21,8 +21,9 @@ MULT = mybir.AluOpType.mult
 P = 128
 PACK = 4
 BANK = 512
+HALF = 256
 SCALAR_NOTES = 256
-VECTOR_RESULT = 384
+VECTOR_RESULT = 416
 
 
 def tile_attend_tab_wideandown_exchange_pl_kernel(
@@ -32,8 +33,8 @@ def tile_attend_tab_wideandown_exchange_pl_kernel(
     with ExitStack() as ctx:
         lists = ctx.enter_context(tc.tile_pool(name="lists", bufs=1))
         sb = ctx.enter_context(tc.tile_pool(name="sb", bufs=1))
-        psum = ctx.enter_context(tc.psum_pool(name="psum", bufs=4))
-        psum_once = ctx.enter_context(tc.psum_pool(name="psum_once", bufs=1))
+        psum = ctx.enter_context(tc.psum_pool(name="psum", bufs=1))
+        banks = [psum.tile([P, BANK], F32, name=f"bank{b}") for b in range(8)]
 
         def quantize(name, woven, width):
             codes = sb.tile([P, width], U32, name=name + "_codes", align_bytes=64)
@@ -46,152 +47,212 @@ def tile_attend_tab_wideandown_exchange_pl_kernel(
         user_list = lists.tile([P, J // 16], U16, name="user_list")
         key_words = sb.tile([P, T], U16, name="key_words")
         key_scales = sb.tile([P, T], U8, name="key_scales")
-        nc.vector.memset(key_scales[:].bitcast(I32), 0)
-        nc.sync.dma_start(out=key_words[:].bitcast(I32), in_=keys_words[0].bitcast(I32))
-        nc.sync.dma_start(token_list[:], offs)
-        for q in range(4):
-            nc.scalar.dma_start(
-                out=key_scales[32 * q : 32 * q + 4, :].bitcast(I32), in_=keys_scales[0, 4 * q : 4 * q + 4, :].bitcast(I32)
-            )
-        nc.sync.dma_start(user_list[:], offs3)
-        nc.sync.dma_start(note_list[:], offs2)
+        nc.gpsimd.memset(key_scales[:].bitcast(I32), 0)
         notes_by_row = notes.rearrange("(p t) u -> p t u", t=PACK)
         users_by_row = users2.rearrange("(p t) z -> p t z", t=PACK)
-        notes_raw = [sb.tile([P, PACK, BANK], F32, name=f"notes_raw{h}") for h in range(U // BANK)]
-        users_raw = [sb.tile([P, Z], F32, name=f"users_raw{t}") for t in range(PACK)]
-        factors = sb.tile([P, PACK], F32, name="factors")
-        nc.sync.dma_start(out=notes_raw[0][:], in_=notes_by_row[:, :, :BANK])
-        nc.sync.dma_start(out=factors[:], in_=rowf.rearrange("(p r) o -> p (r o)", r=PACK))
-        nc.sync.dma_start(out=users_raw[0][:], in_=users_by_row[:, 0, :])
-        nc.sync.dma_start(out=notes_raw[1][:], in_=notes_by_row[:, :, BANK:])
-        for t in range(1, PACK):
-            nc.sync.dma_start(out=users_raw[t][:], in_=users_by_row[:, t, :])
         vals_by_row = vals.rearrange("(m r) t -> m r t", r=PACK)
-        vals_raw = []
+        notes_raw = [sb.tile([P, PACK, HALF], F32, name=f"notes_raw{c}") for c in range(U // HALF)]
+        users_raw = [sb.tile([P, Z], F32, name=f"users_raw{t}") for t in range(PACK)]
+        vals_raw = [sb.tile([P, T], F32, name=f"vals_raw{r}", align_bytes=64) for r in range(PACK)]
+        factors = sb.tile([P, PACK], F32, name="factors")
+        nc.sync.dma_start(token_list[:], offs)
+        for q in range(4):
+            nc.sync.dma_start(
+                out=key_scales[32 * q : 32 * q + 4, :].bitcast(I32), in_=keys_scales[0, 4 * q : 4 * q + 4, :].bitcast(I32)
+            )
+        nc.sync.dma_start(out=key_words[:].bitcast(I32), in_=keys_words[0].bitcast(I32))
+        nc.sync.dma_start(user_list[:], offs3)
+        nc.sync.dma_start(note_list[:], offs2)
+        for c in range(U // HALF):
+            nc.sync.dma_start(out=notes_raw[c][:], in_=notes_by_row[:, :, c * HALF : (c + 1) * HALF])
+        for t in range(PACK):
+            nc.sync.dma_start(out=users_raw[t][:], in_=users_by_row[:, t, :])
+        nc.sync.dma_start(out=factors[:], in_=rowf.rearrange("(p r) o -> p (r o)", r=PACK))
         for r in range(PACK):
-            raw = sb.tile([P, T], F32, name=f"vals_raw{r}", tag=f"vals_raw{r}")
-            nc.sync.dma_start(out=raw[:], in_=vals_by_row[:, r, :])
-            vals_raw.append(raw)
+            nc.sync.dma_start(out=vals_raw[r][:], in_=vals_by_row[:, r, :])
 
         identity = sb.tile([P, P], F32, name="identity")
         make_identity(nc, identity[:])
 
         picked_words = sb.tile([P, I], U16, name="picked_words")
-        nc.vector.tensor_copy(picked_words[:], key_words[:].indirect(token_list[:]))
-        dealt_words = sb.tile([P, PACK, P], U16, name="dealt_words", align_bytes=64)
-        nc.vector.tensor_copy(dealt_words[:], picked_words[:].rearrange("p (s r) -> p r s", r=PACK))
         picked_scales = sb.tile([P, I], U8, name="picked_scales")
-        nc.vector.tensor_copy(picked_scales[:], key_scales[:].indirect(token_list[:]))
+        dealt_words = sb.tile([P, PACK, P], U16, name="dealt_words", align_bytes=64)
         dealt_scales = sb.tile([P, PACK, P], U8, name="dealt_scales", align_bytes=64)
+        nc.vector.tensor_copy(picked_words[:], key_words[:].indirect(token_list[:]))
+        nc.vector.tensor_copy(picked_scales[:], key_scales[:].indirect(token_list[:]))
+        nc.vector.tensor_copy(dealt_words[:], picked_words[:].rearrange("p (s r) -> p r s", r=PACK))
         nc.vector.tensor_copy(dealt_scales[:], picked_scales[:].rearrange("p (s r) -> p r s", r=PACK))
 
-        def keys_product(r, codes, scales):
-            bank = psum.tile([P, BANK], F32, name="bank")
+        def keys_product(out, r, codes, scales):
             nc.tensor.matmul_mx(
-                out=bank[:],
+                out=out,
                 lhsT=dealt_words[:, r, :].bitcast(FP4X4),
                 lhsT_scale=dealt_scales[:, r, :],
-                rhs=codes[:].bitcast(FP8X4),
-                rhs_scale=scales[:],
+                rhs=codes.bitcast(FP8X4),
+                rhs_scale=scales,
                 start=True,
                 stop=True,
             )
-            return bank
 
-        wide = [sb.tile([P, U], F32, name=f"wide{r}") for r in range(PACK)]
-        users_picked = sb.tile([P, PACK, J], BF16, name="users_picked")
-        for h in range(U // BANK):
-            woven = sb.tile([P, BANK, PACK], BF16, name=f"notes_woven{h}", align_bytes=64)
-            turned = notes_raw[h][:].rearrange("p t u -> p u t")
-            split = SCALAR_NOTES if h == 0 else 0
-            if split:
-                nc.scalar.copy(woven[:, :split, :], turned[:, :split, :])
-            nc.vector.tensor_copy(woven[:, split:, :], turned[:, split:, :])
-            codes, scales = quantize(f"notes{h}", woven[:].rearrange("p u t -> p (u t)"), BANK)
-            nc.scalar.activation(users_picked[:, h, :], users_raw[h][:].indirect(user_list[:]), COPY)
+        wide = [sb.tile([P, U], F32, name=f"wide{r}", align_bytes=64) for r in range(PACK)]
+        notes_woven = sb.tile([P, BANK * PACK], BF16, name="notes_woven", tag="staging", align_bytes=64)
+        note_codes = sb.tile([P, U], U32, name="note_codes", align_bytes=64)
+        note_scales = sb.tile([P, U], U8, name="note_scales", align_bytes=64)
+
+        def weave_notes(c, copy):
+            place = notes_woven[:, (c % 2) * HALF * PACK : (c % 2 + 1) * HALF * PACK]
+            copy(place.rearrange("p (u t) -> p u t", t=PACK), notes_raw[c][:].rearrange("p t u -> p u t"))
+
+        def quantize_notes(first, width):
+            start = (first % BANK) * PACK
+            nc.vector.quantize_mx(
+                out=note_codes[:, first : first + width].bitcast(FP8X4),
+                scales=note_scales[:, first : first + width],
+                in_=notes_woven[:, start : start + width * PACK],
+            )
+
+        def wide_columns(first, width):
+            cols = slice(first, first + width)
             for r in range(PACK):
-                bank = keys_product(r, codes, scales)
-                nc.scalar.copy(wide[r][:, h * BANK : (h + 1) * BANK], bank[:])
+                bank = banks[PACK * (first // BANK) + r][:, first % BANK : first % BANK + width]
+                keys_product(bank, r, note_codes[:, cols], note_scales[:, cols])
+                nc.scalar.copy(wide[r][:, cols], bank)
 
-        for t in range(2, PACK):
+        weave_notes(0, nc.scalar.copy)
+        weave_notes(1, nc.scalar.copy)
+        quantize_notes(0, HALF)
+        weave_notes(2, nc.vector.tensor_copy)
+        quantize_notes(HALF, HALF)
+        weave_notes(3, nc.vector.tensor_copy)
+        quantize_notes(BANK, BANK)
+        wide_columns(0, HALF)
+        wide_columns(HALF, HALF)
+        users_picked = sb.tile([P, PACK, J], BF16, name="users_picked", tag="staging", align_bytes=64)
+        nc.scalar.activation(users_picked[:, 0, :], users_raw[0][:].indirect(user_list[:]), COPY)
+        wide_columns(BANK, BANK)
+
+        for t in range(1, PACK):
             nc.vector.tensor_copy(users_picked[:, t, :], users_raw[t][:].indirect(user_list[:]))
         users_woven = sb.tile([P, J, PACK], BF16, name="users_woven", align_bytes=64)
         nc.vector.tensor_copy(users_woven[:], users_picked[:].rearrange("p t j -> p j t"))
         user_codes, user_scales = quantize("users", users_woven[:].rearrange("p j t -> p (j t)"), J)
 
-        table_rows = sb.tile([P, PACK, J], BF16, name="table_rows")
+        table_rows = sb.tile([P, PACK, J], BF16, name="table_rows", align_bytes=64)
+        looked_up = [sb.tile([P, J], F32, name=f"looked_up{r}") for r in range(PACK - 1)]
+        looked_up.append(sb.tile([P, J], F32, name="looked_up_last", tag="staging", align_bytes=64))
+        nc.vector.tensor_copy(looked_up[PACK - 1][:], wide[PACK - 1][:].indirect(note_list[:]))
+        for r in range(PACK - 1):
+            nc.scalar.activation(looked_up[r][:], wide[r][:].indirect(note_list[:]), COPY)
         for r in range(PACK):
-            looked_up = sb.tile([P, J], F32, name=f"looked_up{r}")
-            if r == PACK - 1:
-                nc.vector.tensor_copy(looked_up[:], wide[r][:].indirect(note_list[:]))
-            else:
-                nc.scalar.activation(looked_up[:], wide[r][:].indirect(note_list[:]), COPY)
-            bank = keys_product(r, user_codes, user_scales)
-            larger = sb.tile([P, J], F32, name=f"larger{r}")
-            nc.vector.tensor_tensor(larger[:], looked_up[:], bank[:], MAX)
-            nc.vector.tensor_scalar(table_rows[:, r, :], larger[:], factors[:, r : r + 1], None, MULT)
-        table_woven = sb.tile([P, J, PACK], BF16, name="table_woven", align_bytes=64)
-        nc.vector.tensor_copy(table_woven[:], table_rows[:].rearrange("p r j -> p j r"))
-        table_codes, table_scales = quantize("table", table_woven[:].rearrange("p j r -> p (j r)"), J)
+            keys_product(banks[r][:], r, user_codes[:], user_scales[:])
+        larger = [sb.tile([P, J], F32, name=f"larger{r}", align_bytes=64) for r in range(PACK)]
+        for r in range(PACK):
+            nc.vector.tensor_tensor(larger[r][:], looked_up[r][:], banks[r][:], MAX)
+            if r > 0:
+                nc.vector.tensor_scalar(table_rows[:, r - 1, :], larger[r - 1][:], factors[:, r - 1 : r], None, MULT)
+        nc.vector.tensor_scalar(table_rows[:, PACK - 1, :], larger[PACK - 1][:], factors[:, PACK - 1 :], None, MULT)
+        table_woven = sb.tile([P, J * PACK], BF16, name="table_woven", align_bytes=64)
+        table_codes = sb.tile([P, J], U32, name="table_codes", align_bytes=64)
+        table_scales = sb.tile([P, J], U8, name="table_scales", align_bytes=64)
 
-        val_operands = []
-        for r in range(PACK):
-            vals_picked = sb.tile([P, I], BF16, name=f"vals_picked{r}")
+        def weave_table(h):
+            nc.vector.tensor_copy(
+                table_woven[:, h * HALF * PACK : (h + 1) * HALF * PACK].rearrange("p (j r) -> p j r", r=PACK),
+                table_rows[:, :, h * HALF : (h + 1) * HALF].rearrange("p r j -> p j r"),
+            )
+
+        def quantize_table(h):
+            nc.vector.quantize_mx(
+                out=table_codes[:, h * HALF : (h + 1) * HALF].bitcast(FP8X4),
+                scales=table_scales[:, h * HALF : (h + 1) * HALF],
+                in_=table_woven[:, h * HALF * PACK : (h + 1) * HALF * PACK],
+            )
+
+        val_scales = sb.tile([P, PACK, P], U8, name="val_scales", align_bytes=64)
+        vals_woven = {}
+        val_codes = {}
+
+        def pick_values(r):
+            slot = ("wide2", "vals_raw0")[r % 2]
+            vals_picked = sb.tile([P, I], BF16, name=f"vals_picked{r}", tag=slot, align_bytes=64)
             nc.scalar.activation(vals_picked[:], vals_raw[r][:].indirect(token_list[:]), COPY)
             pairs = vals_picked[:].bitcast(F32)
-            turned = psum_once.tile([P, 2, P], F32, name=f"turned{r}", tag="three_banks" if r == 2 else "one_bank")
             for u in range(2):
-                nc.tensor.transpose(turned[:, u, :], pairs[:, u : I // 2 : 2], identity[:])
-            vals_woven = sb.tile([P, P * PACK], BF16, name=f"vals_woven{r}", align_bytes=64)
-            nc.scalar.copy(
-                vals_woven[:].bitcast(F32).rearrange("p (m u) -> p m u", u=2),
-                turned[:].rearrange("p u m -> p m u"),
-            )
-            val_operands.append(quantize(f"vals{r}", vals_woven[:], P))
+                nc.tensor.transpose(banks[r][:, u * P : (u + 1) * P], pairs[:, u : I // 2 : 2], identity[:])
 
-        result = sb.tile([P, PACK, J], F32, name="result", tag=f"vals_raw{PACK - 1}")
+        def weave_values(r):
+            if r < PACK - 2:
+                alone = sb.tile([P, P * PACK], BF16, name=f"vals_woven{r}", tag=f"vals_raw{r + 1}", align_bytes=64)
+                vals_woven[r] = alone[:]
+            elif r == PACK - 2:
+                both = sb.tile([P, 2 * P * PACK], BF16, name="vals_woven_last", tag=f"vals_raw{r + 1}", align_bytes=64)
+                vals_woven[r] = both[:, : P * PACK]
+                vals_woven[r + 1] = both[:, P * PACK :]
+            nc.scalar.copy(
+                vals_woven[r].bitcast(F32).rearrange("p (m u) -> p m u", u=2),
+                banks[r][:, : 2 * P].rearrange("p (u m) -> p m u", u=2),
+            )
+
+        def quantize_values(pair, slot):
+            codes = sb.tile([P, 2, P], U32, name=f"val_codes{pair}", tag=slot, align_bytes=64)
+            for k in range(2):
+                r = 2 * pair + k
+                val_codes[r] = codes[:, k, :]
+                nc.vector.quantize_mx(out=val_codes[r].bitcast(FP8X4), scales=val_scales[:, r, :], in_=vals_woven[r])
+
+        pick_values(0)
+        for r in range(1, PACK):
+            pick_values(r)
+            weave_values(r - 1)
+        weave_values(PACK - 1)
+        weave_table(0)
+        quantize_values(0, "larger3")
+        quantize_table(0)
+        weave_table(1)
+        quantize_table(1)
+        quantize_values(1, "table_woven")
+
+        result = sb.tile([P, PACK, J], F32, name="result", tag="vals_raw3", align_bytes=64)
         out_by_row = out_0.rearrange("(m r) j -> m r j", r=PACK)
-        early = psum_once.tile([P, PACK - 1, BANK], F32, name="early", tag="three_banks")
-        for r in range(PACK):
-            val_codes, val_scales = val_operands[r]
-            parts = 2 if r == PACK - 1 else 1
-            width = J // parts
-            for part in range(parts):
-                cols = slice(part * width, (part + 1) * width)
-                if parts == 2:
-                    late = psum.tile([P, BANK], F32, name="bank")
-                    bank = late[:, :width]
-                else:
-                    bank = early[:, r, :]
-                nc.tensor.matmul_mx(
-                    out=bank,
-                    lhsT=val_codes[:].bitcast(FP8X4),
-                    lhsT_scale=val_scales[:],
-                    rhs=table_codes[:, cols].bitcast(FP8X4),
-                    rhs_scale=table_scales[:, cols],
-                    start=True,
-                    stop=True,
-                )
-                if r == 1 or (part == 0 and parts == 2):
-                    nc.vector.tensor_copy(result[:, r, cols], bank)
-                else:
-                    nc.scalar.copy(result[:, r, cols], bank)
-            nc.sync.dma_start(out=out_by_row[:, r, :], in_=result[:, r, :])
+        for pair in range(2):
+            for h in range(2):
+                cols = slice(h * HALF, (h + 1) * HALF)
+                for r in (2 * pair, 2 * pair + 1):
+                    bank = banks[PACK * (1 - h) + r][:, :HALF]
+                    nc.tensor.matmul_mx(
+                        out=bank,
+                        lhsT=val_codes[r].bitcast(FP8X4),
+                        lhsT_scale=val_scales[:, r, :],
+                        rhs=table_codes[:, cols].bitcast(FP8X4),
+                        rhs_scale=table_scales[:, cols],
+                        start=True,
+                        stop=True,
+                    )
+                    if pair == 1 and (h == 0 or r == 2):
+                        nc.vector.tensor_copy(result[:, r, cols], bank)
+                    else:
+                        nc.scalar.copy(result[:, r, cols], bank)
+                    if h == 1:
+                        nc.sync.dma_start(out=out_by_row[:, r, :], in_=result[:, r, :])
 
         result_woven = sb.tile([P, J, PACK], BF16, name="result_woven", align_bytes=64)
         result_turned = result[:].rearrange("p r j -> p j r")
         result_codes = sb.tile([P, J], U32, name="result_codes", align_bytes=64)
         result_scales = sb.tile([P, J], U8, name="result_scales", align_bytes=64)
-        nc.vector.tensor_copy(result_woven[:, :256, :], result_turned[:, :256, :])
-        nc.vector.tensor_copy(result_woven[:, 256:VECTOR_RESULT, :], result_turned[:, 256:VECTOR_RESULT, :])
-        nc.scalar.copy(result_woven[:, VECTOR_RESULT:, :], result_turned[:, VECTOR_RESULT:, :])
-        for part in range(2):
-            cols = slice(part * 256, (part + 1) * 256)
+
+        def quantize_result(h):
+            cols = slice(h * HALF, (h + 1) * HALF)
             nc.vector.quantize_mx(
                 out=result_codes[:, cols].bitcast(FP8X4),
                 scales=result_scales[:, cols],
                 in_=result_woven[:, cols, :].rearrange("p j r -> p (j r)"),
             )
+
+        nc.vector.tensor_copy(result_woven[:, :HALF, :], result_turned[:, :HALF, :])
+        nc.vector.tensor_copy(result_woven[:, HALF:VECTOR_RESULT, :], result_turned[:, HALF:VECTOR_RESULT, :])
+        nc.scalar.copy(result_woven[:, VECTOR_RESULT:, :], result_turned[:, VECTOR_RESULT:, :])
+        quantize_result(0)
+        quantize_result(1)
         nc.sync.dma_start(out=out_1[0].rearrange("p c r -> p (c r)").bitcast(I32), in_=result_codes[:].bitcast(I32))
         for q in range(4):
             nc.scalar.dma_start(

@@ -42,18 +42,26 @@ def tile_attend_tab_wideandown_exchange_pl_kernel(
             nc.vector.quantize_mx(out=codes[:].bitcast(FP8X4), scales=scales[:], in_=woven)
             return codes, scales
 
+        def weave(copy, woven, planes):
+            copy(woven.rearrange("p (c i t) -> p c t i", i=4, t=PACK), planes.rearrange("p t (c i) -> p c t i", i=4))
+
+        def deal(dealt, picked, run):
+            nc.vector.tensor_copy(
+                dealt.rearrange("p r (c i) -> p c r i", i=run), picked.rearrange("p (c i r) -> p c r i", i=run, r=PACK)
+            )
+
         token_list = lists.tile([P, I // 16], U16, name="token_list")
         note_list = lists.tile([P, J // 16], U16, name="note_list")
         user_list = lists.tile([P, J // 16], U16, name="user_list")
-        key_words = sb.tile([P, T], U16, name="key_words")
-        key_scales = sb.tile([P, T], U8, name="key_scales")
+        key_words = sb.tile([P, T], U16, name="key_words", align_bytes=256)
+        key_scales = sb.tile([P, T], U8, name="key_scales", align_bytes=256)
         nc.gpsimd.memset(key_scales[:].bitcast(I32), 0)
         notes_by_row = notes.rearrange("(p t) u -> p t u", t=PACK)
         users_by_row = users2.rearrange("(p t) z -> p t z", t=PACK)
         vals_by_row = vals.rearrange("(m r) t -> m r t", r=PACK)
-        notes_raw = [sb.tile([P, PACK, HALF], F32, name=f"notes_raw{c}") for c in range(U // HALF)]
-        users_raw = [sb.tile([P, Z], F32, name=f"users_raw{t}") for t in range(PACK)]
-        vals_raw = [sb.tile([P, T], F32, name=f"vals_raw{r}", align_bytes=64) for r in range(PACK)]
+        notes_raw = [sb.tile([P, PACK, HALF], F32, name=f"notes_raw{c}", align_bytes=256) for c in range(U // HALF)]
+        users_raw = [sb.tile([P, Z], F32, name=f"users_raw{t}", align_bytes=256) for t in range(PACK)]
+        vals_raw = [sb.tile([P, T], F32, name=f"vals_raw{r}", align_bytes=256) for r in range(PACK)]
         factors = sb.tile([P, PACK], F32, name="factors")
         nc.sync.dma_start(token_list[:], offs)
         for q in range(4):
@@ -80,8 +88,8 @@ def tile_attend_tab_wideandown_exchange_pl_kernel(
         dealt_scales = sb.tile([P, PACK, P], U8, name="dealt_scales", align_bytes=64)
         nc.vector.tensor_copy(picked_words[:], key_words[:].indirect(token_list[:]))
         nc.vector.tensor_copy(picked_scales[:], key_scales[:].indirect(token_list[:]))
-        nc.vector.tensor_copy(dealt_words[:], picked_words[:].rearrange("p (s r) -> p r s", r=PACK))
-        nc.vector.tensor_copy(dealt_scales[:], picked_scales[:].rearrange("p (s r) -> p r s", r=PACK))
+        deal(dealt_words[:], picked_words[:], 8)
+        deal(dealt_scales[:], picked_scales[:], 16)
 
         def keys_product(out, r, codes, scales):
             nc.tensor.matmul_mx(
@@ -94,14 +102,14 @@ def tile_attend_tab_wideandown_exchange_pl_kernel(
                 stop=True,
             )
 
-        wide = [sb.tile([P, U], F32, name=f"wide{r}", align_bytes=64) for r in range(PACK)]
+        wide = [sb.tile([P, U], F32, name=f"wide{r}", align_bytes=256) for r in range(PACK)]
         notes_woven = sb.tile([P, BANK * PACK], BF16, name="notes_woven", tag="staging", align_bytes=64)
-        note_codes = sb.tile([P, U], U32, name="note_codes", align_bytes=64)
+        note_codes = sb.tile([P, U], U32, name="note_codes", tag="key_scales", align_bytes=256)
         note_scales = sb.tile([P, U], U8, name="note_scales", align_bytes=64)
 
         def weave_notes(c, copy):
             place = notes_woven[:, (c % 2) * HALF * PACK : (c % 2 + 1) * HALF * PACK]
-            copy(place.rearrange("p (u t) -> p u t", t=PACK), notes_raw[c][:].rearrange("p t u -> p u t"))
+            weave(copy, place, notes_raw[c][:])
 
         def quantize_notes(first, width):
             start = (first % BANK) * PACK
@@ -133,13 +141,13 @@ def tile_attend_tab_wideandown_exchange_pl_kernel(
 
         for t in range(1, PACK):
             nc.vector.tensor_copy(users_picked[:, t, :], users_raw[t][:].indirect(user_list[:]))
-        users_woven = sb.tile([P, J, PACK], BF16, name="users_woven", align_bytes=64)
-        nc.vector.tensor_copy(users_woven[:], users_picked[:].rearrange("p t j -> p j t"))
-        user_codes, user_scales = quantize("users", users_woven[:].rearrange("p j t -> p (j t)"), J)
+        users_woven = sb.tile([P, J * PACK], BF16, name="users_woven", align_bytes=64)
+        weave(nc.vector.tensor_copy, users_woven[:], users_picked[:])
+        user_codes, user_scales = quantize("users", users_woven[:], J)
 
         table_rows = sb.tile([P, PACK, J], BF16, name="table_rows", align_bytes=64)
         looked_up = [sb.tile([P, J], F32, name=f"looked_up{r}") for r in range(PACK - 1)]
-        looked_up.append(sb.tile([P, J], F32, name="looked_up_last", tag="staging", align_bytes=64))
+        looked_up.append(sb.tile([P, J], F32, name="looked_up_last", tag="users_woven", align_bytes=64))
         nc.vector.tensor_copy(looked_up[PACK - 1][:], wide[PACK - 1][:].indirect(note_list[:]))
         for r in range(PACK - 1):
             nc.scalar.activation(looked_up[r][:], wide[r][:].indirect(note_list[:]), COPY)
@@ -151,14 +159,15 @@ def tile_attend_tab_wideandown_exchange_pl_kernel(
             if r > 0:
                 nc.vector.tensor_scalar(table_rows[:, r - 1, :], larger[r - 1][:], factors[:, r - 1 : r], None, MULT)
         nc.vector.tensor_scalar(table_rows[:, PACK - 1, :], larger[PACK - 1][:], factors[:, PACK - 1 :], None, MULT)
-        table_woven = sb.tile([P, J * PACK], BF16, name="table_woven", align_bytes=64)
+        table_woven = sb.tile([P, J * PACK], BF16, name="table_woven", align_bytes=256)
         table_codes = sb.tile([P, J], U32, name="table_codes", align_bytes=64)
         table_scales = sb.tile([P, J], U8, name="table_scales", align_bytes=64)
 
         def weave_table(h):
-            nc.vector.tensor_copy(
-                table_woven[:, h * HALF * PACK : (h + 1) * HALF * PACK].rearrange("p (j r) -> p j r", r=PACK),
-                table_rows[:, :, h * HALF : (h + 1) * HALF].rearrange("p r j -> p j r"),
+            weave(
+                nc.vector.tensor_copy,
+                table_woven[:, h * HALF * PACK : (h + 1) * HALF * PACK],
+                table_rows[:, :, h * HALF : (h + 1) * HALF],
             )
 
         def quantize_table(h):
@@ -168,93 +177,104 @@ def tile_attend_tab_wideandown_exchange_pl_kernel(
                 in_=table_woven[:, h * HALF * PACK : (h + 1) * HALF * PACK],
             )
 
-        val_scales = sb.tile([P, PACK, P], U8, name="val_scales", align_bytes=64)
-        vals_woven = {}
-        val_codes = {}
+        val_scales = sb.tile([P, PACK * P], U8, name="val_scales", align_bytes=64)
+        val_codes = []
+        vals_picked = []
 
-        def pick_values(r):
-            slot = ("wide2", "vals_raw0")[r % 2]
-            vals_picked = sb.tile([P, I], BF16, name=f"vals_picked{r}", tag=slot, align_bytes=64)
-            nc.scalar.activation(vals_picked[:], vals_raw[r][:].indirect(token_list[:]), COPY)
-            pairs = vals_picked[:].bitcast(F32)
+        def pick_values(r, slot):
+            picked = sb.tile([P, I], BF16, name=f"vals_picked{r}", tag=slot, align_bytes=256)
+            vals_picked.append(picked)
+            nc.scalar.activation(picked[:], vals_raw[r][:].indirect(token_list[:]), COPY)
+
+        def turn_values(r, bank):
+            pairs = vals_picked[r][:].bitcast(F32)
             for u in range(2):
-                nc.tensor.transpose(banks[r][:, u * P : (u + 1) * P], pairs[:, u : I // 2 : 2], identity[:])
+                nc.tensor.transpose(bank[:, u * P : (u + 1) * P], pairs[:, u : I // 2 : 2], identity[:])
 
-        def weave_values(r):
-            if r < PACK - 2:
-                alone = sb.tile([P, P * PACK], BF16, name=f"vals_woven{r}", tag=f"vals_raw{r + 1}", align_bytes=64)
-                vals_woven[r] = alone[:]
-            elif r == PACK - 2:
-                both = sb.tile([P, 2 * P * PACK], BF16, name="vals_woven_last", tag=f"vals_raw{r + 1}", align_bytes=64)
-                vals_woven[r] = both[:, : P * PACK]
-                vals_woven[r + 1] = both[:, P * PACK :]
+        def weave_values(woven, turned):
             nc.scalar.copy(
-                vals_woven[r].bitcast(F32).rearrange("p (m u) -> p m u", u=2),
-                banks[r][:, : 2 * P].rearrange("p (u m) -> p m u", u=2),
+                woven.bitcast(F32).rearrange("p (r m u) -> p r m u", m=P, u=2),
+                turned.rearrange("p (r u m) -> p r m u", u=2, m=P),
             )
 
-        def quantize_values(pair, slot):
-            codes = sb.tile([P, 2, P], U32, name=f"val_codes{pair}", tag=slot, align_bytes=64)
-            for k in range(2):
-                r = 2 * pair + k
-                val_codes[r] = codes[:, k, :]
-                nc.vector.quantize_mx(out=val_codes[r].bitcast(FP8X4), scales=val_scales[:, r, :], in_=vals_woven[r])
+        def quantize_values(pair, woven, slot):
+            codes = sb.tile([P, 2 * P], U32, name=f"val_codes{pair}", tag=slot, align_bytes=256)
+            val_codes.append(codes)
+            nc.vector.quantize_mx(
+                out=codes[:].bitcast(FP8X4), scales=val_scales[:, pair * 2 * P : (pair + 1) * 2 * P], in_=woven
+            )
 
-        pick_values(0)
-        for r in range(1, PACK):
-            pick_values(r)
-            weave_values(r - 1)
-        weave_values(PACK - 1)
+        pick_values(0, "wide2")
+        turn_values(0, banks[0][:, :HALF])
+        pick_values(1, "vals_raw0")
+        turn_values(1, banks[0][:, HALF:])
+        pick_values(2, "vals_raw1")
+        turn_values(2, banks[2][:, :HALF])
+        first_pair = sb.tile([P, 2 * P * PACK], BF16, name="first_pair", tag="vals_raw2", align_bytes=256)
+        weave_values(first_pair[:], banks[0][:])
+        pick_values(3, "vals_raw0")
+        turn_values(3, banks[3][:, :HALF])
+        second_pair = sb.tile([P, 2 * P * PACK], BF16, name="second_pair", tag="vals_raw3", align_bytes=256)
+        weave_values(second_pair[:, : P * PACK], banks[2][:, :HALF])
+        weave_values(second_pair[:, P * PACK :], banks[3][:, :HALF])
         weave_table(0)
-        quantize_values(0, "larger3")
-        quantize_table(0)
         weave_table(1)
+        quantize_table(0)
         quantize_table(1)
-        quantize_values(1, "table_woven")
+        quantize_values(0, first_pair[:], "vals_raw0")
+        quantize_values(1, second_pair[:], "table_woven")
 
-        result = sb.tile([P, PACK, J], F32, name="result", tag="vals_raw3", align_bytes=64)
+        result = sb.tile([P, PACK, J], F32, name="result", tag="vals_raw3", align_bytes=256)
         out_by_row = out_0.rearrange("(m r) j -> m r j", r=PACK)
-        for pair in range(2):
-            for h in range(2):
-                cols = slice(h * HALF, (h + 1) * HALF)
-                for r in (2 * pair, 2 * pair + 1):
-                    bank = banks[PACK * (1 - h) + r][:, :HALF]
-                    nc.tensor.matmul_mx(
-                        out=bank,
-                        lhsT=val_codes[r].bitcast(FP8X4),
-                        lhsT_scale=val_scales[:, r, :],
-                        rhs=table_codes[:, cols].bitcast(FP8X4),
-                        rhs_scale=table_scales[:, cols],
-                        start=True,
-                        stop=True,
-                    )
-                    if pair == 1 and (h == 0 or r == 2):
-                        nc.vector.tensor_copy(result[:, r, cols], bank)
-                    else:
-                        nc.scalar.copy(result[:, r, cols], bank)
-                    if h == 1:
-                        nc.sync.dma_start(out=out_by_row[:, r, :], in_=result[:, r, :])
 
-        result_woven = sb.tile([P, J, PACK], BF16, name="result_woven", align_bytes=64)
-        result_turned = result[:].rearrange("p r j -> p j r")
-        result_codes = sb.tile([P, J], U32, name="result_codes", align_bytes=64)
-        result_scales = sb.tile([P, J], U8, name="result_scales", align_bytes=64)
+        def result_product(out, r, h):
+            cols = slice(h * HALF, (h + 1) * HALF)
+            nc.tensor.matmul_mx(
+                out=out,
+                lhsT=val_codes[r // 2][:, (r % 2) * P : (r % 2 + 1) * P].bitcast(FP8X4),
+                lhsT_scale=val_scales[:, r * P : (r + 1) * P],
+                rhs=table_codes[:, cols].bitcast(FP8X4),
+                rhs_scale=table_scales[:, cols],
+                start=True,
+                stop=True,
+            )
 
-        def quantize_result(h):
+        def result_pair(pair, h, bank, copy):
+            for k in range(2):
+                result_product(bank[:, k * HALF : (k + 1) * HALF], 2 * pair + k, h)
+            copy(result[:, 2 * pair : 2 * pair + 2, h * HALF : (h + 1) * HALF], bank[:].rearrange("p (r j) -> p r j", r=2))
+
+        result_pair(0, 0, banks[4], nc.scalar.copy)
+        result_pair(1, 0, banks[5], nc.vector.tensor_copy)
+        result_pair(0, 1, banks[1], nc.scalar.copy)
+        nc.sync.dma_start(out=out_by_row[:, :2, :], in_=result[:, :2, :])
+        result_woven = sb.tile([P, J * PACK], BF16, name="result_woven", align_bytes=64)
+        weave(nc.vector.tensor_copy, result_woven[:, : HALF * PACK], result[:, :, :HALF])
+        result_product(banks[6][:, :HALF], 2, 1)
+        nc.scalar.copy(result[:, 2, HALF:], banks[6][:, :HALF])
+        result_product(banks[7][:, :HALF], 3, 1)
+        nc.scalar.copy(result[:, 3, HALF:], banks[7][:, :HALF])
+        nc.sync.dma_start(out=out_by_row[:, 2:, :], in_=result[:, 2:, :])
+
+        result_codes = sb.tile([P, J], U32, name="result_codes", align_bytes=256)
+        result_scales = sb.tile([P, J], U8, name="result_scales", align_bytes=256)
+        words_out = out_1[0].rearrange("p c r -> p (c r)").bitcast(I32)
+
+        def result_planes(h):
             cols = slice(h * HALF, (h + 1) * HALF)
             nc.vector.quantize_mx(
                 out=result_codes[:, cols].bitcast(FP8X4),
                 scales=result_scales[:, cols],
-                in_=result_woven[:, cols, :].rearrange("p j r -> p (j r)"),
+                in_=result_woven[:, h * HALF * PACK : (h + 1) * HALF * PACK],
             )
+            nc.sync.dma_start(out=words_out[:, cols], in_=result_codes[:, cols].bitcast(I32))
 
-        nc.vector.tensor_copy(result_woven[:, :HALF, :], result_turned[:, :HALF, :])
-        nc.vector.tensor_copy(result_woven[:, HALF:VECTOR_RESULT, :], result_turned[:, HALF:VECTOR_RESULT, :])
-        nc.scalar.copy(result_woven[:, VECTOR_RESULT:, :], result_turned[:, VECTOR_RESULT:, :])
-        quantize_result(0)
-        quantize_result(1)
-        nc.sync.dma_start(out=out_1[0].rearrange("p c r -> p (c r)").bitcast(I32), in_=result_codes[:].bitcast(I32))
+        result_planes(0)
+        weave(nc.vector.tensor_copy, result_woven[:, HALF * PACK : VECTOR_RESULT * PACK], result[:, :, HALF:VECTOR_RESULT])
+        weave(nc.scalar.copy, result_woven[:, VECTOR_RESULT * PACK :], result[:, :, VECTOR_RESULT:])
+        result_planes(1)
         for q in range(4):
-            nc.scalar.dma_start(
+            queue = nc.scalar if q else nc.sync
+            queue.dma_start(
                 out=out_2[0, 4 * q : 4 * q + 4, :].bitcast(I32), in_=result_scales[32 * q : 32 * q + 4, :].bitcast(I32)
             )

@@ -23,7 +23,7 @@ PACK = 4
 BANK = 512
 HALF = 256
 SCALAR_NOTES = 256
-VECTOR_RESULT = 416
+VECTOR_RESULT = 384
 
 
 def tile_attend_tab_wideandown_exchange_pl_kernel(
@@ -69,12 +69,13 @@ def tile_attend_tab_wideandown_exchange_pl_kernel(
                 out=key_scales[32 * q : 32 * q + 4, :].bitcast(I32), in_=keys_scales[0, 4 * q : 4 * q + 4, :].bitcast(I32)
             )
         nc.sync.dma_start(out=key_words[:].bitcast(I32), in_=keys_words[0].bitcast(I32))
+        nc.sync.dma_start(out=notes_raw[0][:], in_=notes_by_row[:, :, :HALF])
         nc.sync.dma_start(user_list[:], offs3)
-        nc.sync.dma_start(note_list[:], offs2)
-        for c in range(U // HALF):
+        for c in range(1, U // HALF):
             nc.sync.dma_start(out=notes_raw[c][:], in_=notes_by_row[:, :, c * HALF : (c + 1) * HALF])
         for t in range(PACK):
             nc.sync.dma_start(out=users_raw[t][:], in_=users_by_row[:, t, :])
+        nc.sync.dma_start(note_list[:], offs2)
         nc.sync.dma_start(out=factors[:], in_=rowf.rearrange("(p r) o -> p (r o)", r=PACK))
         for r in range(PACK):
             nc.sync.dma_start(out=vals_raw[r][:], in_=vals_by_row[:, r, :])
@@ -103,21 +104,19 @@ def tile_attend_tab_wideandown_exchange_pl_kernel(
             )
 
         wide = [sb.tile([P, U], F32, name=f"wide{r}", align_bytes=256) for r in range(PACK)]
-        notes_woven = sb.tile([P, BANK * PACK], BF16, name="notes_woven", tag="staging", align_bytes=64)
         note_codes = sb.tile([P, U], U32, name="note_codes", tag="key_scales", align_bytes=256)
         note_scales = sb.tile([P, U], U8, name="note_scales", align_bytes=64)
+        notes_woven = []
 
         def weave_notes(c, copy):
-            place = notes_woven[:, (c % 2) * HALF * PACK : (c % 2 + 1) * HALF * PACK]
-            weave(copy, place, notes_raw[c][:])
+            slot = f"notes_woven{c}" if c < 2 else f"notes_raw{c - 2}"
+            woven = sb.tile([P, HALF * PACK], BF16, name=f"notes_woven{c}", tag=slot, align_bytes=256)
+            notes_woven.append(woven)
+            weave(copy, woven[:], notes_raw[c][:])
 
-        def quantize_notes(first, width):
-            start = (first % BANK) * PACK
-            nc.vector.quantize_mx(
-                out=note_codes[:, first : first + width].bitcast(FP8X4),
-                scales=note_scales[:, first : first + width],
-                in_=notes_woven[:, start : start + width * PACK],
-            )
+        def quantize_notes(c):
+            cols = slice(c * HALF, (c + 1) * HALF)
+            nc.vector.quantize_mx(out=note_codes[:, cols].bitcast(FP8X4), scales=note_scales[:, cols], in_=notes_woven[c][:])
 
         def wide_columns(first, width):
             cols = slice(first, first + width)
@@ -128,14 +127,15 @@ def tile_attend_tab_wideandown_exchange_pl_kernel(
 
         weave_notes(0, nc.scalar.copy)
         weave_notes(1, nc.scalar.copy)
-        quantize_notes(0, HALF)
+        quantize_notes(0)
         weave_notes(2, nc.vector.tensor_copy)
-        quantize_notes(HALF, HALF)
+        quantize_notes(1)
         weave_notes(3, nc.vector.tensor_copy)
-        quantize_notes(BANK, BANK)
+        quantize_notes(2)
+        quantize_notes(3)
         wide_columns(0, HALF)
         wide_columns(HALF, HALF)
-        users_picked = sb.tile([P, PACK, J], BF16, name="users_picked", tag="staging", align_bytes=64)
+        users_picked = sb.tile([P, PACK, J], BF16, name="users_picked", tag="notes_raw3", align_bytes=256)
         nc.scalar.activation(users_picked[:, 0, :], users_raw[0][:].indirect(user_list[:]), COPY)
         wide_columns(BANK, BANK)
 
@@ -145,9 +145,9 @@ def tile_attend_tab_wideandown_exchange_pl_kernel(
         weave(nc.vector.tensor_copy, users_woven[:], users_picked[:])
         user_codes, user_scales = quantize("users", users_woven[:], J)
 
-        table_rows = sb.tile([P, PACK, J], BF16, name="table_rows", align_bytes=64)
+        table_rows = sb.tile([P, PACK, J], BF16, name="table_rows", align_bytes=256)
         looked_up = [sb.tile([P, J], F32, name=f"looked_up{r}") for r in range(PACK - 1)]
-        looked_up.append(sb.tile([P, J], F32, name="looked_up_last", tag="users_woven", align_bytes=64))
+        looked_up.append(sb.tile([P, J], F32, name="looked_up_last", tag="notes_raw3", align_bytes=256))
         nc.vector.tensor_copy(looked_up[PACK - 1][:], wide[PACK - 1][:].indirect(note_list[:]))
         for r in range(PACK - 1):
             nc.scalar.activation(looked_up[r][:], wide[r][:].indirect(note_list[:]), COPY)
@@ -204,27 +204,27 @@ def tile_attend_tab_wideandown_exchange_pl_kernel(
                 out=codes[:].bitcast(FP8X4), scales=val_scales[:, pair * 2 * P : (pair + 1) * 2 * P], in_=woven
             )
 
-        pick_values(0, "wide2")
+        pick_values(0, "wide1")
         turn_values(0, banks[0][:, :HALF])
-        pick_values(1, "vals_raw0")
+        pick_values(1, "wide2")
         turn_values(1, banks[0][:, HALF:])
-        pick_values(2, "vals_raw1")
+        pick_values(2, "vals_raw0")
         turn_values(2, banks[2][:, :HALF])
-        first_pair = sb.tile([P, 2 * P * PACK], BF16, name="first_pair", tag="vals_raw2", align_bytes=256)
-        weave_values(first_pair[:], banks[0][:])
-        pick_values(3, "vals_raw0")
+        pick_values(3, "vals_raw1")
         turn_values(3, banks[3][:, :HALF])
-        second_pair = sb.tile([P, 2 * P * PACK], BF16, name="second_pair", tag="vals_raw3", align_bytes=256)
-        weave_values(second_pair[:, : P * PACK], banks[2][:, :HALF])
-        weave_values(second_pair[:, P * PACK :], banks[3][:, :HALF])
+        vals_woven = sb.tile([P, PACK * P * PACK], BF16, name="vals_woven", tag="vals_raw3", align_bytes=256)
+        tile_width = P * PACK
+        weave_values(vals_woven[:, : 2 * tile_width], banks[0][:])
+        weave_values(vals_woven[:, 2 * tile_width : 3 * tile_width], banks[2][:, :HALF])
+        weave_values(vals_woven[:, 3 * tile_width :], banks[3][:, :HALF])
         weave_table(0)
         weave_table(1)
         quantize_table(0)
+        quantize_values(0, vals_woven[:, : 2 * tile_width], "table_rows")
         quantize_table(1)
-        quantize_values(0, first_pair[:], "vals_raw0")
-        quantize_values(1, second_pair[:], "table_woven")
+        quantize_values(1, vals_woven[:, 2 * tile_width :], "table_woven")
 
-        result = sb.tile([P, PACK, J], F32, name="result", tag="vals_raw3", align_bytes=256)
+        result = sb.tile([P, PACK, J], F32, name="result", align_bytes=256)
         out_by_row = out_0.rearrange("(m r) j -> m r j", r=PACK)
 
         def result_product(out, r, h):

from contextlib import ExitStack

import concourse.mybir as mybir
from concourse.masks import make_identity

D, T, I, J, U, Z, E = 512, 2048, 512, 512, 1024, 1024, 512
FLOPS = 2 * D * I * U + 2 * D * I * J + 2 * I * E * J

F32 = mybir.dt.float32
BF16 = mybir.dt.bfloat16
I32 = mybir.dt.int32
U32 = mybir.dt.uint32
U16 = mybir.dt.uint16
U8 = mybir.dt.uint8
FP8X4 = mybir.dt.float8_e4m3fn_x4
FP4X4 = mybir.dt.float4_e2m1fn_x4
COPY = mybir.ActivationFunctionType.Copy
MAX = mybir.AluOpType.max
MULT = mybir.AluOpType.mult

P = 128
PACK = 4
BANK = 512
HALF = 256
SCALAR_NOTES = 256
VECTOR_RESULT = 384


def tile_attend_tab_wideandown_exchange_pl_kernel(
    tc, keys_words, keys_scales, notes, users2, rowf, vals, offs, offs2, offs3, out_0, out_1, out_2
):
    nc = tc.nc
    with ExitStack() as ctx:
        lists = ctx.enter_context(tc.tile_pool(name="lists", bufs=1))
        sb = ctx.enter_context(tc.tile_pool(name="sb", bufs=1))
        psum = ctx.enter_context(tc.psum_pool(name="psum", bufs=1))
        banks = [psum.tile([P, BANK], F32, name=f"bank{b}") for b in range(8)]

        def quantize(name, woven, width):
            codes = sb.tile([P, width], U32, name=name + "_codes", align_bytes=64)
            scales = sb.tile([P, width], U8, name=name + "_scales", align_bytes=64)
            nc.vector.quantize_mx(out=codes[:].bitcast(FP8X4), scales=scales[:], in_=woven)
            return codes, scales

        def weave(copy, woven, planes):
            copy(woven.rearrange("p (c i t) -> p c t i", i=4, t=PACK), planes.rearrange("p t (c i) -> p c t i", i=4))

        def deal(dealt, picked, run):
            nc.vector.tensor_copy(
                dealt.rearrange("p r (c i) -> p c r i", i=run), picked.rearrange("p (c i r) -> p c r i", i=run, r=PACK)
            )

        token_list = lists.tile([P, I // 16], U16, name="token_list")
        note_list = lists.tile([P, J // 16], U16, name="note_list")
        user_list = lists.tile([P, J // 16], U16, name="user_list")
        key_words = sb.tile([P, T], U16, name="key_words", align_bytes=256)
        key_scales = sb.tile([P, T], U8, name="key_scales", align_bytes=256)
        nc.gpsimd.memset(key_scales[:].bitcast(I32), 0)
        notes_by_row = notes.rearrange("(p t) u -> p t u", t=PACK)
        users_by_row = users2.rearrange("(p t) z -> p t z", t=PACK)
        vals_by_row = vals.rearrange("(m r) t -> m r t", r=PACK)
        notes_raw = [sb.tile([P, PACK, HALF], F32, name=f"notes_raw{c}", align_bytes=256) for c in range(U // HALF)]
        users_raw = [sb.tile([P, Z], F32, name=f"users_raw{t}", align_bytes=256) for t in range(PACK)]
        vals_raw = [sb.tile([P, T], F32, name=f"vals_raw{r}", align_bytes=256) for r in range(PACK)]
        factors = sb.tile([P, PACK], F32, name="factors")
        nc.sync.dma_start(token_list[:], offs)
        for q in range(4):
            nc.sync.dma_start(
                out=key_scales[32 * q : 32 * q + 4, :].bitcast(I32), in_=keys_scales[0, 4 * q : 4 * q + 4, :].bitcast(I32)
            )
        nc.sync.dma_start(out=key_words[:].bitcast(I32), in_=keys_words[0].bitcast(I32))
        nc.sync.dma_start(out=notes_raw[0][:], in_=notes_by_row[:, :, :HALF])
        nc.sync.dma_start(user_list[:], offs3)
        for c in range(1, U // HALF):
            nc.sync.dma_start(out=notes_raw[c][:], in_=notes_by_row[:, :, c * HALF : (c + 1) * HALF])
        for t in range(PACK):
            nc.sync.dma_start(out=users_raw[t][:], in_=users_by_row[:, t, :])
        nc.sync.dma_start(note_list[:], offs2)
        nc.sync.dma_start(out=factors[:], in_=rowf.rearrange("(p r) o -> p (r o)", r=PACK))
        for r in range(PACK):
            nc.sync.dma_start(out=vals_raw[r][:], in_=vals_by_row[:, r, :])

        identity = sb.tile([P, P], F32, name="identity")
        make_identity(nc, identity[:])

        picked_words = sb.tile([P, I], U16, name="picked_words")
        picked_scales = sb.tile([P, I], U8, name="picked_scales")
        dealt_words = sb.tile([P, PACK, P], U16, name="dealt_words", align_bytes=64)
        dealt_scales = sb.tile([P, PACK, P], U8, name="dealt_scales", align_bytes=64)
        nc.vector.tensor_copy(picked_words[:], key_words[:].indirect(token_list[:]))
        nc.vector.tensor_copy(picked_scales[:], key_scales[:].indirect(token_list[:]))
        deal(dealt_words[:], picked_words[:], 8)
        deal(dealt_scales[:], picked_scales[:], 16)

        def keys_product(out, r, codes, scales):
            nc.tensor.matmul_mx(
                out=out,
                lhsT=dealt_words[:, r, :].bitcast(FP4X4),
                lhsT_scale=dealt_scales[:, r, :],
                rhs=codes.bitcast(FP8X4),
                rhs_scale=scales,
                start=True,
                stop=True,
            )

        wide = [sb.tile([P, U], F32, name=f"wide{r}", align_bytes=256) for r in range(PACK)]
        note_codes = sb.tile([P, U], U32, name="note_codes", tag="key_scales", align_bytes=256)
        note_scales = sb.tile([P, U], U8, name="note_scales", align_bytes=64)
        notes_woven = []

        def weave_notes(c, copy):
            slot = f"notes_woven{c}" if c < 2 else f"notes_raw{c - 2}"
            woven = sb.tile([P, HALF * PACK], BF16, name=f"notes_woven{c}", tag=slot, align_bytes=256)
            notes_woven.append(woven)
            weave(copy, woven[:], notes_raw[c][:])

        def quantize_notes(c):
            cols = slice(c * HALF, (c + 1) * HALF)
            nc.vector.quantize_mx(out=note_codes[:, cols].bitcast(FP8X4), scales=note_scales[:, cols], in_=notes_woven[c][:])

        def wide_columns(first, width):
            cols = slice(first, first + width)
            for r in range(PACK):
                bank = banks[PACK * (first // BANK) + r][:, first % BANK : first % BANK + width]
                keys_product(bank, r, note_codes[:, cols], note_scales[:, cols])
                nc.scalar.copy(wide[r][:, cols], bank)

        weave_notes(0, nc.scalar.copy)
        weave_notes(1, nc.scalar.copy)
        quantize_notes(0)
        weave_notes(2, nc.vector.tensor_copy)
        quantize_notes(1)
        weave_notes(3, nc.vector.tensor_copy)
        quantize_notes(2)
        quantize_notes(3)
        wide_columns(0, HALF)
        wide_columns(HALF, HALF)
        users_picked = sb.tile([P, PACK, J], BF16, name="users_picked", tag="notes_raw3", align_bytes=256)
        nc.scalar.activation(users_picked[:, 0, :], users_raw[0][:].indirect(user_list[:]), COPY)
        wide_columns(BANK, BANK)

        for t in range(1, PACK):
            nc.vector.tensor_copy(users_picked[:, t, :], users_raw[t][:].indirect(user_list[:]))
        users_woven = sb.tile([P, J * PACK], BF16, name="users_woven", align_bytes=64)
        weave(nc.vector.tensor_copy, users_woven[:], users_picked[:])
        user_codes, user_scales = quantize("users", users_woven[:], J)

        table_rows = sb.tile([P, PACK, J], BF16, name="table_rows", align_bytes=256)
        looked_up = [sb.tile([P, J], F32, name=f"looked_up{r}") for r in range(PACK - 1)]
        looked_up.append(sb.tile([P, J], F32, name="looked_up_last", tag="notes_raw3", align_bytes=256))
        nc.vector.tensor_copy(looked_up[PACK - 1][:], wide[PACK - 1][:].indirect(note_list[:]))
        for r in range(PACK - 1):
            nc.scalar.activation(looked_up[r][:], wide[r][:].indirect(note_list[:]), COPY)
        for r in range(PACK):
            keys_product(banks[r][:], r, user_codes[:], user_scales[:])
        larger = [sb.tile([P, J], F32, name=f"larger{r}", align_bytes=64) for r in range(PACK)]
        for r in range(PACK):
            nc.vector.tensor_tensor(larger[r][:], looked_up[r][:], banks[r][:], MAX)
            if r > 0:
                nc.vector.tensor_scalar(table_rows[:, r - 1, :], larger[r - 1][:], factors[:, r - 1 : r], None, MULT)
        nc.vector.tensor_scalar(table_rows[:, PACK - 1, :], larger[PACK - 1][:], factors[:, PACK - 1 :], None, MULT)
        table_woven = sb.tile([P, J * PACK], BF16, name="table_woven", align_bytes=256)
        table_codes = sb.tile([P, J], U32, name="table_codes", align_bytes=64)
        table_scales = sb.tile([P, J], U8, name="table_scales", align_bytes=64)

        def weave_table(h):
            weave(
                nc.vector.tensor_copy,
                table_woven[:, h * HALF * PACK : (h + 1) * HALF * PACK],
                table_rows[:, :, h * HALF : (h + 1) * HALF],
            )

        def quantize_table(h):
            nc.vector.quantize_mx(
                out=table_codes[:, h * HALF : (h + 1) * HALF].bitcast(FP8X4),
                scales=table_scales[:, h * HALF : (h + 1) * HALF],
                in_=table_woven[:, h * HALF * PACK : (h + 1) * HALF * PACK],
            )

        val_scales = sb.tile([P, PACK * P], U8, name="val_scales", align_bytes=64)
        val_codes = []
        vals_picked = []

        def pick_values(r, slot):
            picked = sb.tile([P, I], BF16, name=f"vals_picked{r}", tag=slot, align_bytes=256)
            vals_picked.append(picked)
            nc.scalar.activation(picked[:], vals_raw[r][:].indirect(token_list[:]), COPY)

        def turn_values(r, bank):
            pairs = vals_picked[r][:].bitcast(F32)
            for u in range(2):
                nc.tensor.transpose(bank[:, u * P : (u + 1) * P], pairs[:, u : I // 2 : 2], identity[:])

        def weave_values(woven, turned):
            nc.scalar.copy(
                woven.bitcast(F32).rearrange("p (r m u) -> p r m u", m=P, u=2),
                turned.rearrange("p (r u m) -> p r m u", u=2, m=P),
            )

        def quantize_values(pair, woven, slot):
            codes = sb.tile([P, 2 * P], U32, name=f"val_codes{pair}", tag=slot, align_bytes=256)
            val_codes.append(codes)
            nc.vector.quantize_mx(
                out=codes[:].bitcast(FP8X4), scales=val_scales[:, pair * 2 * P : (pair + 1) * 2 * P], in_=woven
            )

        pick_values(0, "wide1")
        turn_values(0, banks[0][:, :HALF])
        pick_values(1, "wide2")
        turn_values(1, banks[0][:, HALF:])
        pick_values(2, "vals_raw0")
        turn_values(2, banks[2][:, :HALF])
        pick_values(3, "vals_raw1")
        turn_values(3, banks[3][:, :HALF])
        vals_woven = sb.tile([P, PACK * P * PACK], BF16, name="vals_woven", tag="vals_raw3", align_bytes=256)
        tile_width = P * PACK
        weave_values(vals_woven[:, : 2 * tile_width], banks[0][:])
        weave_values(vals_woven[:, 2 * tile_width : 3 * tile_width], banks[2][:, :HALF])
        weave_values(vals_woven[:, 3 * tile_width :], banks[3][:, :HALF])
        weave_table(0)
        weave_table(1)
        quantize_table(0)
        quantize_values(0, vals_woven[:, : 2 * tile_width], "table_rows")
        quantize_table(1)
        quantize_values(1, vals_woven[:, 2 * tile_width :], "table_woven")

        result = sb.tile([P, PACK, J], F32, name="result", align_bytes=256)
        out_by_row = out_0.rearrange("(m r) j -> m r j", r=PACK)

        def result_product(out, r, h):
            cols = slice(h * HALF, (h + 1) * HALF)
            nc.tensor.matmul_mx(
                out=out,
                lhsT=val_codes[r // 2][:, (r % 2) * P : (r % 2 + 1) * P].bitcast(FP8X4),
                lhsT_scale=val_scales[:, r * P : (r + 1) * P],
                rhs=table_codes[:, cols].bitcast(FP8X4),
                rhs_scale=table_scales[:, cols],
                start=True,
                stop=True,
            )

        def result_pair(pair, h, bank, copy):
            for k in range(2):
                result_product(bank[:, k * HALF : (k + 1) * HALF], 2 * pair + k, h)
            copy(result[:, 2 * pair : 2 * pair + 2, h * HALF : (h + 1) * HALF], bank[:].rearrange("p (r j) -> p r j", r=2))

        result_pair(0, 0, banks[4], nc.scalar.copy)
        result_pair(1, 0, banks[5], nc.vector.tensor_copy)
        result_pair(0, 1, banks[1], nc.scalar.copy)
        nc.sync.dma_start(out=out_by_row[:, :2, :], in_=result[:, :2, :])
        result_woven = sb.tile([P, J * PACK], BF16, name="result_woven", align_bytes=64)
        weave(nc.vector.tensor_copy, result_woven[:, : HALF * PACK], result[:, :, :HALF])
        result_product(banks[6][:, :HALF], 2, 1)
        nc.scalar.copy(result[:, 2, HALF:], banks[6][:, :HALF])
        result_product(banks[7][:, :HALF], 3, 1)
        nc.scalar.copy(result[:, 3, HALF:], banks[7][:, :HALF])
        nc.sync.dma_start(out=out_by_row[:, 2:, :], in_=result[:, 2:, :])

        result_codes = sb.tile([P, J], U32, name="result_codes", align_bytes=256)
        result_scales = sb.tile([P, J], U8, name="result_scales", align_bytes=256)
        words_out = out_1[0].rearrange("p c r -> p (c r)").bitcast(I32)

        def result_planes(h):
            cols = slice(h * HALF, (h + 1) * HALF)
            nc.vector.quantize_mx(
                out=result_codes[:, cols].bitcast(FP8X4),
                scales=result_scales[:, cols],
                in_=result_woven[:, h * HALF * PACK : (h + 1) * HALF * PACK],
            )
            nc.sync.dma_start(out=words_out[:, cols], in_=result_codes[:, cols].bitcast(I32))

        result_planes(0)
        weave(nc.vector.tensor_copy, result_woven[:, HALF * PACK : VECTOR_RESULT * PACK], result[:, :, HALF:VECTOR_RESULT])
        weave(nc.scalar.copy, result_woven[:, VECTOR_RESULT * PACK :], result[:, :, VECTOR_RESULT:])
        result_planes(1)
        for q in range(4):
            queue = nc.scalar if q else nc.sync
            queue.dma_start(
                out=out_2[0, 4 * q : 4 * q + 4, :].bitcast(I32), in_=result_scales[32 * q : 32 * q + 4, :].bitcast(I32)
            )
